import numpy as np
import ml_dtypes


def mxq(x, axis, fmt="e4m3"):
    dtype, down = {"e4m3": (ml_dtypes.float8_e4m3fn, 7), "e5m2": (ml_dtypes.float8_e5m2, 14)}[fmt]
    v = np.moveaxis(np.asarray(x, np.float32).astype(ml_dtypes.bfloat16).astype(np.float64), axis, -1)
    blocks = v.reshape(v.shape[:-1] + (-1, 32))
    amax = np.abs(blocks).max(-1, keepdims=True)
    byte = np.maximum(np.where(amax > 0, np.frexp(amax)[1] - 1 + 127, 0) - down, 1)
    scale = np.exp2(byte - 127.0)
    codes = (blocks / scale).astype(np.float32).astype(dtype).astype(np.float64)
    return np.moveaxis((codes * scale).reshape(v.shape), -1, axis)


WIDE = False


def mx_kscale(k):
    if not WIDE:
        return np.ones(k)
    levels = np.array([10, -10, 5, -5, 0])
    if k % 512:
        return np.exp2(np.random.permutation(np.resize(levels, k // 32))).repeat(32)
    a = np.empty((k // 512, 16))
    for p in range(k // 512):
        a[p, :8] = np.random.permutation(np.resize(levels, 8))
        for g in range(8):
            far = levels[np.abs(levels - a[p, g]) >= 10]
            a[p, g + 8] = far[np.random.randint(len(far))]
    return np.exp2(a.ravel()).repeat(32)


BF16 = ml_dtypes.bfloat16


def bf(x):
    return np.asarray(x, np.float32).astype(BF16)


def f64(x):
    return np.asarray(x).astype(np.float64)


E2M1 = np.array([0.0, 0.5, 1.0, 1.5, 2.0, 3.0, 4.0, 6.0, -0.0, -0.5, -1.0, -1.5, -2.0, -3.0, -4.0, -6.0])


def pack_weight(w, fmt):
    k, n = w.shape
    w = f64(bf(w)).reshape(k // 32, 32, n)
    amax = np.abs(w).max(1)
    if fmt == "e4m3":
        byte = np.frexp(amax)[1] - 1 + 127 - 7
    else:
        mant, ex = np.frexp(amax / 6.0)
        byte = np.where(mant > 0.5, ex, ex - 1) + 127
    byte = np.clip(np.where(amax > 0, byte, 1), 1, 254)
    scaled = (w * np.exp2(127.0 - byte)[:, None, :]).reshape(k, n).astype(np.float32)
    by_word = np.ascontiguousarray(scaled.reshape(k // 512, 128, 4, n).transpose(0, 1, 3, 2))
    if fmt == "e4m3":
        words = by_word.astype(ml_dtypes.float8_e4m3fn).view(np.uint8)
    else:
        c = by_word.astype(ml_dtypes.float4_e2m1fn).view(np.uint8) & 0xF
        words = c[..., 0::2] | (c[..., 1::2] << 4)
    return np.ascontiguousarray(words), np.ascontiguousarray(byte.astype(np.uint8).reshape(k // 512, 16, n))


def unpack_weight(words, scales, fmt):
    g, p, n, _ = words.shape
    if fmt == "e4m3":
        vals = np.ascontiguousarray(words).view(ml_dtypes.float8_e4m3fn).astype(np.float64)
    else:
        nib = np.empty((g, p, n, 4), np.uint8)
        nib[..., 0::2] = words & 0xF
        nib[..., 1::2] = words >> 4
        vals = E2M1[nib]
    vals = vals * np.repeat(np.exp2(scales.astype(np.float64) - 127.0), 8, axis=1)[..., None]
    return vals.transpose(0, 1, 3, 2).reshape(g * 512, n)
def pack4(w):
    words, scales = pack_weight(w, "e2m1")
    return words.reshape(words.shape[0], 128, -1), scales


def unpack4(words, scales):
    return unpack_weight(words.reshape(words.shape[0], 128, -1, 2), scales, "e2m1")


S, C, U, L = 1024, 2048, 512, 2048

NORMAL = 2.0
TOP = 4


def setup_inputs():
    s = mx_kscale(C)
    r = mx_kscale(U)
    geno = np.minimum(np.random.poisson(0.8, (C, L)), TOP) / s[:, None]
    geno_words, geno_scales = pack4(geno)
    return {
        "d_known": bf(np.random.standard_normal((S, C)) / np.sqrt(C) * s),
        "geno_words": geno_words,
        "geno_scales": geno_scales,
        "d_new": bf(np.random.standard_normal((S, U)) / np.sqrt(U) * r),
        "geno_new": bf(np.random.exponential(0.8, (U, L)) / r[:, None]),
        "purity": bf(np.random.uniform(0.3, 0.9, (S,))),
        "cn_excess": bf(np.random.randint(-1, 4, (L,))),
    }


def reference(d_known, geno_words, geno_scales, d_new, geno_new, purity, cn_excess):
    geno = unpack4(geno_words, geno_scales)
    known = mxq(f64(d_known), 1, "e4m3") @ geno
    new = mxq(f64(d_new), 1, "e4m3") @ mxq(f64(geno_new), 0, "e4m3")
    mutated = known + new
    rho = f64(purity)[:, None]
    copies = NORMAL + rho * f64(cn_excess)[None, :]
    return rho * mutated / copies

@@ -1,0 +1,364 @@
+from contextlib import ExitStack
+
+import concourse.mybir as mybir
+from concourse.masks import make_identity
+
+S, C, U, L = 1024, 2048, 512, 2048
+FLOPS = 2 * S * (C + U) * L
+
+F32 = mybir.dt.float32
+BF16 = mybir.dt.bfloat16
+I32 = mybir.dt.int32
+U32 = mybir.dt.uint32
+U8 = mybir.dt.uint8
+FP8X4 = mybir.dt.float8_e4m3fn_x4
+FP4X4 = mybir.dt.float4_e2m1fn_x4
+ALU = mybir.AluOpType
+ACT = mybir.ActivationFunctionType
+AXIS = mybir.AxisListType
+
+P = 128
+N = 512
+ROWS = S // P
+COLS = L // N
+KNOWN_PASSES = C // 512
+NORMAL = 2.0
+
+
+def tile_clone_allele_shift_s1_kernel(
+    tc, d_known, geno_words, geno_scales, d_new, geno_new, purity, cn_excess, out
+):
+    nc = tc.nc
+    known_rows = d_known.rearrange("(p t) k -> t p k", t=ROWS)
+    new_rows = d_new.rearrange("(p t) k -> p (t k)", t=ROWS)
+    out_rows = out.rearrange("(p t) n -> t p n", t=ROWS)
+
+    with ExitStack() as ctx:
+        keep = ctx.enter_context(tc.tile_pool(name="keep", bufs=1))
+        work = ctx.enter_context(tc.tile_pool(name="work", bufs=3))
+        psum = ctx.enter_context(tc.psum_pool(name="psum", bufs=1))
+        ctx.enter_context(tc.manual_schedule())
+
+        free_banks = list(range(8))
+
+        def take_bank():
+            b = free_banks[0]
+            free_banks.remove(b)
+            return b, psum.tile([P, N], F32, name="bank%d" % b, tag="bank%d" % b)
+
+        def kept(name, shape, dtype):
+            return keep.tile(shape, dtype, name=name, tag=name, align_bytes=64)
+
+        cn = kept("cn", [P, 16], BF16)
+        rho = kept("rho", [P, ROWS], BF16)
+        nc.scalar.dma_start(out=cn[:], in_=cn_excess.rearrange("(p m) -> p m", p=P))
+        nc.scalar.dma_start(out=rho[:], in_=purity.rearrange("(p t) -> p t", p=P))
+        ident = kept("ident", [P, P], F32)
+        make_identity(nc, ident[:])
+
+        g_scales = []
+        for n in range(COLS):
+            plane = kept("g_scales%d" % n, [P, KNOWN_PASSES, N], U8)
+            nc.vector.memset(plane[:].bitcast(I32), 0)
+            g_scales.append(plane)
+
+        raw = {}
+        g_words = {}
+        n_raw = {}
+
+        def load_rows(name, src):
+            raw[name] = kept("raw_%s" % name, [P, src.shape[1]], BF16)
+            nc.sync.dma_start(out=raw[name][:], in_=src)
+
+        def load_g(n):
+            for r in range(4):
+                src = geno_scales[:, r:16:4, N * n : N * (n + 1)].rearrange("g q n -> q g n")
+                nc.sync.dma_start(out=g_scales[n][r:P:32, :, :].bitcast(I32), in_=src.bitcast(I32))
+            g_words[n] = kept("g_words%d" % n, [P, KNOWN_PASSES, 2 * N], U8)
+            src = geno_words[:, :, 2 * N * n : 2 * N * (n + 1)].rearrange("g p b -> p g b")
+            nc.sync.dma_start(out=g_words[n][:].bitcast(I32), in_=src.bitcast(I32))
+
+        def load_geno_new(n):
+            n_raw[n] = kept("n_raw%d" % n, [P, 4, N], BF16)
+            nc.sync.dma_start(
+                out=n_raw[n][:], in_=geno_new[:, N * n : N * (n + 1)].rearrange("(p j) w -> p j w", j=4)
+            )
+
+        load_rows("k0", known_rows[0])
+        load_rows("k1", known_rows[1])
+        load_g(0)
+        load_g(1)
+        load_rows("k2", known_rows[2])
+        load_rows("n0", new_rows[:, 0:2048])
+        load_geno_new(0)
+        load_geno_new(1)
+        load_rows("k3", known_rows[3])
+        load_geno_new(2)
+        load_g(2)
+        load_rows("k4", known_rows[4])
+        load_rows("k5", known_rows[5])
+        load_rows("n1", new_rows[:, 2048:4096])
+        load_geno_new(3)
+        load_g(3)
+        load_rows("k6", known_rows[6])
+        load_rows("k7", known_rows[7])
+
+        ordered = {}
+        turned = {}
+        grouped = {}
+        codes = {}
+        scales = {}
+
+        def order_words(name, units):
+            width = 512 * len(units)
+            tile = work.tile([P, width], F32, name="ordered", tag="ordered", bufs=4)
+            nc.vector.tensor_copy(
+                out=tile[:].rearrange("p (g u c i) -> p g c u i", u=2, c=32, i=4),
+                in_=raw[name][:].bitcast(F32).rearrange("p (g c i u) -> p g c u i", u=2, c=32, i=4),
+            )
+            for i, unit in enumerate(units):
+                ordered[unit] = tile[:, 512 * i : 512 * (i + 1)]
+
+        def turn(unit):
+            b, bank = take_bank()
+            for q in range(4):
+                nc.tensor.transpose(bank[:, P * q : P * (q + 1)], ordered[unit][:, P * q : P * (q + 1)], ident[:])
+            turned[unit] = (b, bank)
+
+        def gather(unit, on_vector=False):
+            b, bank = turned[unit]
+            tile = work.tile([P, 1024], BF16, name="grouped", tag="grouped", bufs=6, align_bytes=64)
+            dst = tile[:].bitcast(F32).rearrange("p (g m u) -> p g m u", g=2, u=2)
+            src = bank[:].rearrange("p (g u m) -> p g m u", g=2, u=2)
+            if on_vector:
+                nc.vector.tensor_copy(out=dst, in_=src)
+            else:
+                nc.scalar.copy(out=dst, in_=src)
+            grouped[unit] = tile
+            free_banks.append(b)
+
+        def quantise(unit):
+            words = grouped[unit].shape[1] // 4
+            codes[unit] = kept("codes_%s" % unit, [P, words], U32)
+            scales[unit] = kept("scales_%s" % unit, [P, words], U8)
+            nc.vector.quantize_mx(out=codes[unit][:].bitcast(FP8X4), scales=scales[unit][:], in_=grouped[unit][:])
+
+        def interleave_geno_new(n):
+            tile = work.tile([P, 4 * N], BF16, name="n_grouped", tag="n_grouped", bufs=2, align_bytes=64)
+            nc.vector.tensor_copy(
+                out=tile[:].rearrange("p (c i j) -> p c j i", i=4, j=4),
+                in_=n_raw[n][:].rearrange("p j (c i) -> p c j i", i=4),
+            )
+            grouped["g%d" % n] = tile
+
+        groups = {}
+
+        def known_passes(t, n, lo=0, width=N):
+            groups[t, n, lo] = take_bank()
+            acc = groups[t, n, lo][1]
+            for g in range(KNOWN_PASSES):
+                unit = "k%d%s" % (t, "ab"[g // 2])
+                cols = slice(P * (g % 2), P * (g % 2 + 1))
+                nc.tensor.matmul_mx(
+                    out=acc[:, 0:width],
+                    lhsT=codes[unit][:, cols].bitcast(FP8X4),
+                    lhsT_scale=scales[unit][:, cols],
+                    rhs=g_words[n][:, g, 2 * lo : 2 * (lo + width)].bitcast(FP4X4),
+                    rhs_scale=g_scales[n][:, g, lo : lo + width],
+                    start=(g == 0),
+                    stop=False,
+                )
+
+        def new_pass(t, n, lo=0, width=N):
+            unit = "n%d" % (t // 2)
+            cols = slice(P * (t % 2), P * (t % 2 + 1))
+            nc.tensor.matmul_mx(
+                out=groups[t, n, lo][1][:, 0:width],
+                lhsT=codes[unit][:, cols].bitcast(FP8X4),
+                lhsT_scale=scales[unit][:, cols],
+                rhs=codes["g%d" % n][:, lo : lo + width].bitcast(FP8X4),
+                rhs_scale=scales["g%d" % n][:, lo : lo + width],
+                start=False,
+                stop=True,
+            )
+
+        shares = {}
+
+        def share(t, n):
+            tile = work.tile([P, N], F32, name="share", tag="share", bufs=8)
+            nc.scalar.activation(
+                out=tile[:], in_=ln_b[:, N * n : N * (n + 1)], func=ACT.Sigmoid, scale=-1.0, bias=ln_a[:, t : t + 1]
+            )
+            shares[t, n] = tile
+
+        def finish(t, n, lo=0, width=N):
+            b, acc = groups[t, n, lo]
+            res = work.tile([P, width], F32, name="res", tag="res", bufs=16)
+            nc.vector.scalar_tensor_tensor(
+                out=res[:],
+                in0=acc[:, 0:width],
+                scalar=inv_a[:, t : t + 1],
+                in1=shares[t, n][:, lo : lo + width],
+                op0=ALU.mult,
+                op1=ALU.mult,
+            )
+            free_banks.append(b)
+            nc.sync.dma_start(out=out_rows[t][:, N * n + lo : N * n + lo + width], in_=res[:])
+
+        cn_low_here = kept("cn_low_here", [P, 1], F32)
+        nc.vector.tensor_reduce(out=cn_low_here[:], in_=cn[:], axis=AXIS.X, op=ALU.min)
+        inv_rho = kept("inv_rho", [P, ROWS], F32)
+        nc.vector.reciprocal(out=inv_rho[:], in_=rho[:])
+        low_b, low_bank = take_bank()
+        nc.tensor.transpose(low_bank[:, 0:P], cn_low_here[:, 0:1].to_broadcast([P, P]), ident[:])
+        cn_words = cn[:].bitcast(F32)
+        cn_banks = []
+        for h in range(2):
+            b, bank = take_bank()
+            for m in range(4):
+                word = cn_words[:, 4 * h + m : 4 * h + m + 1].to_broadcast([P, P])
+                nc.tensor.transpose(bank[:, P * m : P * (m + 1)], word, ident[:])
+            cn_banks.append((b, bank))
+        inv_rho_low = kept("inv_rho_low", [P, 1], F32)
+        nc.vector.tensor_reduce(out=inv_rho_low[:], in_=inv_rho[:], axis=AXIS.X, op=ALU.min)
+
+        order_words("k0", ["k0a", "k0b"])
+        turn("k0a")
+        turn("k0b")
+        cn_low = kept("cn_low", [P, 1], F32)
+        nc.vector.tensor_reduce(out=cn_low[:], in_=low_bank[:, 0:P], axis=AXIS.X, op=ALU.min)
+        free_banks.append(low_b)
+        shift = kept("shift", [P, 1], F32)
+        nc.vector.scalar_tensor_tensor(
+            out=shift[:], in0=cn_low[:], scalar=-0.5, in1=inv_rho_low[:], op0=ALU.mult, op1=ALU.add
+        )
+        a = kept("a", [P, ROWS], F32)
+        nc.vector.tensor_scalar(
+            out=a[:], in0=inv_rho[:], scalar1=NORMAL, scalar2=shift[:, 0:1], op0=ALU.mult, op1=ALU.subtract
+        )
+        ln_a = kept("ln_a", [P, ROWS], F32)
+        nc.scalar.activation(out=ln_a[:], in_=a[:], func=ACT.Ln)
+        order_words("k1", ["k1a", "k1b"])
+        turn("k1a")
+        turn("k1b")
+        gather("k0a")
+        gather("k0b")
+        ln_b = kept("ln_b", [P, L], F32)
+        for h in range(2):
+            b, bank = cn_banks[h]
+            nc.scalar.activation(
+                out=ln_b[:].rearrange("q (p m e) -> q p m e", m=8, e=2)[:, :, 4 * h : 4 * h + 4, :],
+                in_=bank[:].bitcast(BF16).rearrange("q (m p e) -> q p m e", m=4, e=2),
+                func=ACT.Ln,
+                bias=shift[:, 0:1],
+            )
+            free_banks.append(b)
+        share(0, 0)
+        quantise("k0a")
+        gather("k1a", on_vector=True)
+        quantise("k0b")
+        gather("k1b", on_vector=True)
+        quantise("k1a")
+        quantise("k1b")
+        inv_a = kept("inv_a", [P, ROWS], F32)
+        nc.vector.reciprocal(out=inv_a[:], in_=a[:])
+        known_passes(0, 0)
+        known_passes(1, 0)
+        known_passes(0, 1)
+        order_words("k2", ["k2a", "k2b"])
+        turn("k2a")
+        turn("k2b")
+        gather("k2a")
+        gather("k2b")
+        share(1, 0)
+        share(2, 0)
+        order_words("n0", ["n0", "n1"])
+        quantise("k2a")
+        quantise("k2b")
+        known_passes(1, 1)
+        turn("n0")
+        turn("n1")
+        gather("n0")
+        gather("n1")
+        share(0, 1)
+        share(1, 1)
+        share(2, 1)
+        interleave_geno_new(0)
+        quantise("n0")
+        quantise("n1")
+        quantise("g0")
+        interleave_geno_new(1)
+        order_words("k3", ["k3a", "k3b"])
+        quantise("g1")
+        known_passes(2, 0)
+        known_passes(2, 1)
+        turn("k3a")
+        turn("k3b")
+        gather("k3a")
+        gather("k3b")
+        interleave_geno_new(2)
+        closed = []
+        for n in range(2):
+            for t in range(3):
+                new_pass(t, n)
+                closed.append((t, n))
+        finish(*closed[0])
+        closed.remove(closed[0])
+        quantise("k3a")
+        quantise("k3b")
+        quantise("g2")
+
+        order = [(3, 0), (3, 1)]
+        order.extend((t, 2) for t in range(4))
+        order.extend((t, n) for t in (4, 5) for n in range(3))
+        order.extend((t, 3) for t in range(6))
+        order.extend((t, n) for t in (6, 7) for n in range(COLS))
+        col3 = order.index((0, 3))
+        share(*order[0])
+        share(*order[1])
+        for i, (t, n) in enumerate(order[:-1]):
+            for row in (4, 6):
+                first = order.index((row, 0))
+                units = ["k%da" % row, "k%db" % row, "n%d" % (row // 2), "k%da" % (row + 1), "k%db" % (row + 1)]
+                if i == first - 2:
+                    for unit in units:
+                        turn(unit)
+                    for unit in units[:3]:
+                        gather(unit)
+                if i == first - 1:
+                    for unit in units[:3]:
+                        quantise(unit)
+                    for unit in units[3:]:
+                        gather(unit)
+                if i == first + 1:
+                    for unit in units[3:]:
+                        quantise(unit)
+            known_passes(t, n)
+            new_pass(t, n)
+            for g in closed[:2]:
+                finish(*g)
+                closed.remove(g)
+            closed.append((t, n))
+            if i + 2 < len(order):
+                share(*order[i + 2])
+            for row in (4, 6):
+                first = order.index((row, 0))
+                if i == first - 5:
+                    order_words("k%d" % row, ["k%da" % row, "k%db" % row])
+                if i == first - 4:
+                    order_words("k%d" % (row + 1), ["k%da" % (row + 1), "k%db" % (row + 1)])
+                if row == 4 and i == first - 3:
+                    order_words("n1", ["n2", "n3"])
+            if i == col3 - 3:
+                interleave_geno_new(3)
+            if i == col3 - 2:
+                quantise("g3")
+        t, n = order[-1]
+        for lo in range(0, N, P):
+            known_passes(t, n, lo, P)
+            new_pass(t, n, lo, P)
+            for g in closed[:]:
+                finish(*g)
+                closed.remove(g)
+            closed.append((t, n, lo, P))
+        finish(*closed[0])

@@ -23,6 +23,9 @@ ROWS = S // P
 COLS = L // N
 KNOWN_PASSES = C // 512
 NORMAL = 2.0
+G2AT = (2, 0)
+SPLIT = 84
+SPLIT2 = 64
 
 
 def tile_clone_allele_shift_s1_kernel(
@@ -89,17 +92,17 @@ def tile_clone_allele_shift_s1_kernel(
         load_g(0)
         load_g(1)
         load_rows("k2", known_rows[2])
-        load_rows("n0", new_rows[:, 0:2048])
         load_geno_new(0)
-        load_geno_new(1)
+        load_rows("n0", new_rows[:, 0:2048])
         load_rows("k3", known_rows[3])
+        load_geno_new(1)
         load_geno_new(2)
         load_g(2)
         load_rows("k4", known_rows[4])
-        load_rows("k5", known_rows[5])
         load_rows("n1", new_rows[:, 2048:4096])
         load_geno_new(3)
         load_g(3)
+        load_rows("k5", known_rows[5])
         load_rows("k6", known_rows[6])
         load_rows("k7", known_rows[7])
 
@@ -109,10 +112,10 @@ def tile_clone_allele_shift_s1_kernel(
         codes = {}
         scales = {}
 
-        def order_words(name, units):
+        def order_words(name, units, on_scalar=False):
             width = 512 * len(units)
             tile = work.tile([P, width], F32, name="ordered", tag="ordered", bufs=4)
-            nc.vector.tensor_copy(
+            (nc.scalar.copy if on_scalar else nc.vector.tensor_copy)(
                 out=tile[:].rearrange("p (g u c i) -> p g c u i", u=2, c=32, i=4),
                 in_=raw[name][:].bitcast(F32).rearrange("p (g c i u) -> p g c u i", u=2, c=32, i=4),
             )
@@ -143,12 +146,14 @@ def tile_clone_allele_shift_s1_kernel(
             scales[unit] = kept("scales_%s" % unit, [P, words], U8)
             nc.vector.quantize_mx(out=codes[unit][:].bitcast(FP8X4), scales=scales[unit][:], in_=grouped[unit][:])
 
-        def interleave_geno_new(n):
+        def interleave_geno_new(n, split):
             tile = work.tile([P, 4 * N], BF16, name="n_grouped", tag="n_grouped", bufs=2, align_bytes=64)
-            nc.vector.tensor_copy(
-                out=tile[:].rearrange("p (c i j) -> p c j i", i=4, j=4),
-                in_=n_raw[n][:].rearrange("p j (c i) -> p c j i", i=4),
-            )
+            dst = tile[:].rearrange("p (c i j) -> p c j i", i=4, j=4)
+            src = n_raw[n][:].rearrange("p j (c i) -> p c j i", i=4)
+            if split > 0:
+                nc.vector.tensor_copy(out=dst[:, 0:split], in_=src[:, 0:split])
+            if split < N // 4:
+                nc.scalar.copy(out=dst[:, split:], in_=src[:, split:])
             grouped["g%d" % n] = tile
 
         groups = {}
@@ -222,9 +227,6 @@ def tile_clone_allele_shift_s1_kernel(
         inv_rho_low = kept("inv_rho_low", [P, 1], F32)
         nc.vector.tensor_reduce(out=inv_rho_low[:], in_=inv_rho[:], axis=AXIS.X, op=ALU.min)
 
-        order_words("k0", ["k0a", "k0b"])
-        turn("k0a")
-        turn("k0b")
         cn_low = kept("cn_low", [P, 1], F32)
         nc.vector.tensor_reduce(out=cn_low[:], in_=low_bank[:, 0:P], axis=AXIS.X, op=ALU.min)
         free_banks.append(low_b)
@@ -232,17 +234,11 @@ def tile_clone_allele_shift_s1_kernel(
         nc.vector.scalar_tensor_tensor(
             out=shift[:], in0=cn_low[:], scalar=-0.5, in1=inv_rho_low[:], op0=ALU.mult, op1=ALU.add
         )
+        order_words("k0", ["k0a", "k0b"])
         a = kept("a", [P, ROWS], F32)
         nc.vector.tensor_scalar(
             out=a[:], in0=inv_rho[:], scalar1=NORMAL, scalar2=shift[:, 0:1], op0=ALU.mult, op1=ALU.subtract
         )
-        ln_a = kept("ln_a", [P, ROWS], F32)
-        nc.scalar.activation(out=ln_a[:], in_=a[:], func=ACT.Ln)
-        order_words("k1", ["k1a", "k1b"])
-        turn("k1a")
-        turn("k1b")
-        gather("k0a")
-        gather("k0b")
         ln_b = kept("ln_b", [P, L], F32)
         for h in range(2):
             b, bank = cn_banks[h]
@@ -253,15 +249,26 @@ def tile_clone_allele_shift_s1_kernel(
                 bias=shift[:, 0:1],
             )
             free_banks.append(b)
-        share(0, 0)
+        ln_a = kept("ln_a", [P, ROWS], F32)
+        nc.scalar.activation(out=ln_a[:], in_=a[:], func=ACT.Ln)
+        turn("k0a")
+        turn("k0b")
+        order_words("k1", ["k1a", "k1b"])
+        turn("k1a")
+        turn("k1b")
+        gather("k0a", on_vector=True)
+        gather("k0b")
+        inv_a = kept("inv_a", [P, ROWS], F32)
+        nc.vector.reciprocal(out=inv_a[:], in_=a[:])
         quantise("k0a")
         gather("k1a", on_vector=True)
         quantise("k0b")
         gather("k1b", on_vector=True)
         quantise("k1a")
         quantise("k1b")
-        inv_a = kept("inv_a", [P, ROWS], F32)
-        nc.vector.reciprocal(out=inv_a[:], in_=a[:])
+        for n in range(2):
+            for t in range(3):
+                share(t, n)
         known_passes(0, 0)
         known_passes(1, 0)
         known_passes(0, 1)
@@ -270,87 +277,76 @@ def tile_clone_allele_shift_s1_kernel(
         turn("k2b")
         gather("k2a")
         gather("k2b")
-        share(1, 0)
-        share(2, 0)
+        interleave_geno_new(0, N // 4)
         order_words("n0", ["n0", "n1"])
         quantise("k2a")
         quantise("k2b")
+        quantise("g0")
         known_passes(1, 1)
         turn("n0")
         turn("n1")
         gather("n0")
         gather("n1")
-        share(0, 1)
-        share(1, 1)
-        share(2, 1)
-        interleave_geno_new(0)
-        quantise("n0")
-        quantise("n1")
-        quantise("g0")
-        interleave_geno_new(1)
-        order_words("k3", ["k3a", "k3b"])
-        quantise("g1")
         known_passes(2, 0)
         known_passes(2, 1)
+        order_words("k3", ["k3a", "k3b"])
+        quantise("n0")
+        interleave_geno_new(1, SPLIT)
+        quantise("n1")
+        quantise("g1")
         turn("k3a")
         turn("k3b")
         gather("k3a")
         gather("k3b")
-        interleave_geno_new(2)
+        interleave_geno_new(2, SPLIT2)
         closed = []
         for n in range(2):
             for t in range(3):
                 new_pass(t, n)
                 closed.append((t, n))
+        quantise("k3a")
         finish(*closed[0])
         closed.remove(closed[0])
-        quantise("k3a")
         quantise("k3b")
-        quantise("g2")
 
         order = [(3, 0), (3, 1)]
         order.extend((t, 2) for t in range(4))
-        order.extend((t, n) for t in (4, 5) for n in range(3))
-        order.extend((t, 3) for t in range(6))
-        order.extend((t, n) for t in (6, 7) for n in range(COLS))
+        order.extend((4, n) for n in range(3))
+        order.extend((t, 3) for t in range(5))
+        order.extend((t, n) for t in range(5, ROWS) for n in range(COLS))
         col3 = order.index((0, 3))
         share(*order[0])
         share(*order[1])
         for i, (t, n) in enumerate(order[:-1]):
-            for row in (4, 6):
+            for row in range(4, ROWS):
                 first = order.index((row, 0))
-                units = ["k%da" % row, "k%db" % row, "n%d" % (row // 2), "k%da" % (row + 1), "k%db" % (row + 1)]
+                units = ["k%da" % row, "k%db" % row] + (["n%d" % (row // 2)] if row % 2 == 0 else [])
                 if i == first - 2:
                     for unit in units:
                         turn(unit)
-                    for unit in units[:3]:
+                    for unit in units:
                         gather(unit)
                 if i == first - 1:
-                    for unit in units[:3]:
-                        quantise(unit)
-                    for unit in units[3:]:
-                        gather(unit)
-                if i == first + 1:
-                    for unit in units[3:]:
+                    for unit in units:
                         quantise(unit)
             known_passes(t, n)
             new_pass(t, n)
             for g in closed[:2]:
                 finish(*g)
                 closed.remove(g)
+                if g == G2AT:
+                    quantise("g2")
             closed.append((t, n))
             if i + 2 < len(order):
                 share(*order[i + 2])
-            for row in (4, 6):
+            for row in range(4, ROWS):
                 first = order.index((row, 0))
-                if i == first - 5:
-                    order_words("k%d" % row, ["k%da" % row, "k%db" % row])
                 if i == first - 4:
-                    order_words("k%d" % (row + 1), ["k%da" % (row + 1), "k%db" % (row + 1)])
+                    order_words("k%d" % row, ["k%da" % row, "k%db" % row], on_scalar=(row == 4))
                 if row == 4 and i == first - 3:
-                    order_words("n1", ["n2", "n3"])
+                    order_words("n1", ["n2", "n3"], on_scalar=True)
             if i == col3 - 3:
-                interleave_geno_new(3)
+                interleave_geno_new(3, N // 4)
             if i == col3 - 2:
                 quantise("g3")
         t, n = order[-1]

@@ -18,14 +18,20 @@ ACT = mybir.ActivationFunctionType
 AXIS = mybir.AxisListType
 
 P = 128
+QUADRANT = 32
+BANKS = 8
 N = 512
 ROWS = S // P
 COLS = L // N
 KNOWN_PASSES = C // 512
+PAIR_WORDS = 512
 NORMAL = 2.0
-G2AT = (2, 0)
-SPLIT = 84
-SPLIT2 = 64
+
+RUNS = N // 4
+VECTOR_RUNS = (RUNS, 84, 64, RUNS)
+VECTOR_ROWS = (ROWS - 2, ROWS - 1)
+SPARE_STEPS = 2
+RESULT_BUFS = 22
 
 
 def tile_clone_allele_shift_s1_kernel(
@@ -42,17 +48,17 @@ def tile_clone_allele_shift_s1_kernel(
         psum = ctx.enter_context(tc.psum_pool(name="psum", bufs=1))
         ctx.enter_context(tc.manual_schedule())
 
-        free_banks = list(range(8))
+        free_banks = list(range(BANKS))
 
         def take_bank():
-            b = free_banks[0]
-            free_banks.remove(b)
-            return b, psum.tile([P, N], F32, name="bank%d" % b, tag="bank%d" % b)
+            number = free_banks[0]
+            free_banks.remove(number)
+            return number, psum.tile([P, N], F32, name="bank%d" % number, tag="bank%d" % number)
 
         def kept(name, shape, dtype):
             return keep.tile(shape, dtype, name=name, tag=name, align_bytes=64)
 
-        cn = kept("cn", [P, 16], BF16)
+        cn = kept("cn", [P, L // P], BF16)
         rho = kept("rho", [P, ROWS], BF16)
         nc.scalar.dma_start(out=cn[:], in_=cn_excess.rearrange("(p m) -> p m", p=P))
         nc.scalar.dma_start(out=rho[:], in_=purity.rearrange("(p t) -> p t", p=P))
@@ -61,300 +67,345 @@ def tile_clone_allele_shift_s1_kernel(
 
         g_scales = []
         for n in range(COLS):
-            plane = kept("g_scales%d" % n, [P, KNOWN_PASSES, N], U8)
-            nc.vector.memset(plane[:].bitcast(I32), 0)
-            g_scales.append(plane)
+            scale_tile = kept("g_scales%d" % n, [P, KNOWN_PASSES, N], U8)
+            nc.vector.memset(scale_tile[:].bitcast(I32), 0)
+            g_scales.append(scale_tile)
 
-        raw = {}
-        g_words = {}
-        n_raw = {}
+        known_raw = {}
+        new_raw = {}
+        g_codes = {}
+        geno_new_raw = {}
 
-        def load_rows(name, src):
-            raw[name] = kept("raw_%s" % name, [P, src.shape[1]], BF16)
-            nc.sync.dma_start(out=raw[name][:], in_=src)
+        def load_known(t):
+            known_raw[t] = kept("known_raw%d" % t, [P, C], BF16)
+            nc.sync.dma_start(out=known_raw[t][:], in_=known_rows[t])
+
+        def load_new(half):
+            new_raw[half] = kept("new_raw%d" % half, [P, 4 * U], BF16)
+            nc.sync.dma_start(out=new_raw[half][:], in_=new_rows[:, 4 * U * half : 4 * U * (half + 1)])
 
         def load_g(n):
             for r in range(4):
-                src = geno_scales[:, r:16:4, N * n : N * (n + 1)].rearrange("g q n -> q g n")
-                nc.sync.dma_start(out=g_scales[n][r:P:32, :, :].bitcast(I32), in_=src.bitcast(I32))
-            g_words[n] = kept("g_words%d" % n, [P, KNOWN_PASSES, 2 * N], U8)
-            src = geno_words[:, :, 2 * N * n : 2 * N * (n + 1)].rearrange("g p b -> p g b")
-            nc.sync.dma_start(out=g_words[n][:].bitcast(I32), in_=src.bitcast(I32))
+                rows = geno_scales[:, r:16:4, N * n : N * (n + 1)].rearrange("g q n -> q g n")
+                nc.sync.dma_start(out=g_scales[n][r:P:QUADRANT, :, :].bitcast(I32), in_=rows.bitcast(I32))
+            g_codes[n] = kept("g_codes%d" % n, [P, KNOWN_PASSES, 2 * N], U8)
+            words = geno_words[:, :, 2 * N * n : 2 * N * (n + 1)].rearrange("g p b -> p g b")
+            nc.sync.dma_start(out=g_codes[n][:].bitcast(I32), in_=words.bitcast(I32))
 
         def load_geno_new(n):
-            n_raw[n] = kept("n_raw%d" % n, [P, 4, N], BF16)
-            nc.sync.dma_start(
-                out=n_raw[n][:], in_=geno_new[:, N * n : N * (n + 1)].rearrange("(p j) w -> p j w", j=4)
-            )
+            geno_new_raw[n] = kept("geno_new_raw%d" % n, [P, 4, N], BF16)
+            rows = geno_new[:, N * n : N * (n + 1)].rearrange("(p j) w -> p j w", j=4)
+            nc.sync.dma_start(out=geno_new_raw[n][:], in_=rows)
 
-        load_rows("k0", known_rows[0])
-        load_rows("k1", known_rows[1])
+        load_known(0)
+        load_known(1)
         load_g(0)
         load_g(1)
-        load_rows("k2", known_rows[2])
+        load_known(2)
         load_geno_new(0)
-        load_rows("n0", new_rows[:, 0:2048])
-        load_rows("k3", known_rows[3])
+        load_new(0)
+        load_known(3)
         load_geno_new(1)
         load_geno_new(2)
         load_g(2)
-        load_rows("k4", known_rows[4])
-        load_rows("n1", new_rows[:, 2048:4096])
+        load_known(4)
+        load_new(1)
         load_geno_new(3)
         load_g(3)
-        load_rows("k5", known_rows[5])
-        load_rows("k6", known_rows[6])
-        load_rows("k7", known_rows[7])
+        load_known(5)
+        by_quadrant = kept("by_quadrant", [P, 4, 2 * KNOWN_PASSES, P], BF16)
+        pieces = d_known.rearrange("(i b t) (g q k) -> b q i (t g) k", b=4, t=ROWS, q=4, k=P)
+        for b in range(4):
+            for q in (0, 2, 1, 3):
+                nc.sync.dma_start(
+                    out=by_quadrant[QUADRANT * q : QUADRANT * (q + 1), b, :, :],
+                    in_=pieces[b, q][:, KNOWN_PASSES * VECTOR_ROWS[0] :, :],
+                )
 
-        ordered = {}
+        sorted_words = {}
         turned = {}
         grouped = {}
         codes = {}
         scales = {}
 
-        def order_words(name, units, on_scalar=False):
-            width = 512 * len(units)
-            tile = work.tile([P, width], F32, name="ordered", tag="ordered", bufs=4)
-            (nc.scalar.copy if on_scalar else nc.vector.tensor_copy)(
+        def known_pairs(t):
+            return [("known", t, 0), ("known", t, 1)]
+
+        def new_pairs(half):
+            return [("new", 2 * half), ("new", 2 * half + 1)]
+
+        def sort_words(raw, pairs, copy):
+            tile = work.tile([P, 2 * PAIR_WORDS], F32, name="sorted", tag="sorted", bufs=3, align_bytes=64)
+            copy(
                 out=tile[:].rearrange("p (g u c i) -> p g c u i", u=2, c=32, i=4),
-                in_=raw[name][:].bitcast(F32).rearrange("p (g c i u) -> p g c u i", u=2, c=32, i=4),
+                in_=raw[:].bitcast(F32).rearrange("p (g c i u) -> p g c u i", u=2, c=32, i=4),
             )
-            for i, unit in enumerate(units):
-                ordered[unit] = tile[:, 512 * i : 512 * (i + 1)]
+            for place, pair in enumerate(pairs):
+                sorted_words[pair] = tile[:, PAIR_WORDS * place : PAIR_WORDS * (place + 1)]
 
-        def turn(unit):
-            b, bank = take_bank()
-            for q in range(4):
-                nc.tensor.transpose(bank[:, P * q : P * (q + 1)], ordered[unit][:, P * q : P * (q + 1)], ident[:])
-            turned[unit] = (b, bank)
+        def turn(pair):
+            number, bank = take_bank()
+            for x in range(4):
+                nc.tensor.transpose(bank[:, P * x : P * (x + 1)], sorted_words[pair][:, P * x : P * (x + 1)], ident[:])
+            turned[pair] = (number, bank)
 
-        def gather(unit, on_vector=False):
-            b, bank = turned[unit]
-            tile = work.tile([P, 1024], BF16, name="grouped", tag="grouped", bufs=6, align_bytes=64)
-            dst = tile[:].bitcast(F32).rearrange("p (g m u) -> p g m u", g=2, u=2)
-            src = bank[:].rearrange("p (g u m) -> p g m u", g=2, u=2)
-            if on_vector:
-                nc.vector.tensor_copy(out=dst, in_=src)
-            else:
-                nc.scalar.copy(out=dst, in_=src)
-            grouped[unit] = tile
-            free_banks.append(b)
+        def group_tile():
+            return work.tile([P, 2 * PAIR_WORDS], BF16, name="grouped", tag="grouped", bufs=6, align_bytes=64)
 
-        def quantise(unit):
-            words = grouped[unit].shape[1] // 4
-            codes[unit] = kept("codes_%s" % unit, [P, words], U32)
-            scales[unit] = kept("scales_%s" % unit, [P, words], U8)
-            nc.vector.quantize_mx(out=codes[unit][:].bitcast(FP8X4), scales=scales[unit][:], in_=grouped[unit][:])
+        def regroup(pair, copy):
+            number, bank = turned[pair]
+            grouped[pair] = group_tile()
+            copy(
+                out=grouped[pair][:].bitcast(F32).rearrange("p (g m u) -> p g m u", g=2, u=2),
+                in_=bank[:].rearrange("p (g u m) -> p g m u", g=2, u=2),
+            )
+            free_banks.append(number)
 
-        def interleave_geno_new(n, split):
-            tile = work.tile([P, 4 * N], BF16, name="n_grouped", tag="n_grouped", bufs=2, align_bytes=64)
+        def sort_blocks(pair):
+            place, half = VECTOR_ROWS.index(pair[1]), pair[2]
+            tile = work.tile([P, PAIR_WORDS], F32, name="sorted_blocks", tag="sorted_blocks", align_bytes=64)
+            words = by_quadrant[:].rearrange("p b x k -> p (b x k)").bitcast(F32)
+            words = words.rearrange("p (b v g j u) -> p v g b u j", b=4, v=2, g=KNOWN_PASSES, u=2)
+            nc.scalar.copy(
+                out=tile[:].rearrange("p (g b u j) -> p g b u j", g=2, b=4, u=2),
+                in_=words[:, place, 2 * half : 2 * half + 2],
+            )
+            sorted_words[pair] = tile
+
+        def turn_blocks(pair):
+            turned[pair] = work.tile([P, PAIR_WORDS], F32, name="turned_blocks", tag="turned_blocks", align_bytes=64)
+            nc.vector.transpose(out=turned[pair][:], in_=sorted_words[pair][:])
+
+        def regroup_blocks(pair):
+            grouped[pair] = group_tile()
+            nc.scalar.copy(
+                out=grouped[pair][:].bitcast(F32).rearrange("p (g i c x) -> p g c i x", g=2, c=2, x=4),
+                in_=turned[pair][:].rearrange("p (g c x i) -> p g c i x", g=2, c=2, x=4),
+            )
+
+        def interleave_geno_new(n):
+            tile = work.tile([P, 4 * N], BF16, name="interleaved", tag="interleaved", bufs=2, align_bytes=64)
             dst = tile[:].rearrange("p (c i j) -> p c j i", i=4, j=4)
-            src = n_raw[n][:].rearrange("p j (c i) -> p c j i", i=4)
-            if split > 0:
-                nc.vector.tensor_copy(out=dst[:, 0:split], in_=src[:, 0:split])
-            if split < N // 4:
+            src = geno_new_raw[n][:].rearrange("p j (c i) -> p c j i", i=4)
+            split = VECTOR_RUNS[n]
+            nc.vector.tensor_copy(out=dst[:, 0:split], in_=src[:, 0:split])
+            if split < RUNS:
                 nc.scalar.copy(out=dst[:, split:], in_=src[:, split:])
-            grouped["g%d" % n] = tile
+            grouped["geno_new", n] = tile
 
-        groups = {}
+        def quantise(key):
+            columns = grouped[key].shape[1] // 4
+            name = "_".join(str(part) for part in key)
+            codes[key] = kept("codes_" + name, [P, columns], U32)
+            scales[key] = kept("scales_" + name, [P, columns], U8)
+            nc.vector.quantize_mx(out=codes[key][:].bitcast(FP8X4), scales=scales[key][:], in_=grouped[key][:])
 
-        def known_passes(t, n, lo=0, width=N):
-            groups[t, n, lo] = take_bank()
-            acc = groups[t, n, lo][1]
+        sums = {}
+        sigmoids = {}
+
+        def known_passes(t, n, first=0, width=N):
+            sums[t, n, first] = take_bank()
             for g in range(KNOWN_PASSES):
-                unit = "k%d%s" % (t, "ab"[g // 2])
-                cols = slice(P * (g % 2), P * (g % 2 + 1))
+                pair = ("known", t, g // 2)
+                samples = slice(P * (g % 2), P * (g % 2 + 1))
                 nc.tensor.matmul_mx(
-                    out=acc[:, 0:width],
-                    lhsT=codes[unit][:, cols].bitcast(FP8X4),
-                    lhsT_scale=scales[unit][:, cols],
-                    rhs=g_words[n][:, g, 2 * lo : 2 * (lo + width)].bitcast(FP4X4),
-                    rhs_scale=g_scales[n][:, g, lo : lo + width],
+                    out=sums[t, n, first][1][:, 0:width],
+                    lhsT=codes[pair][:, samples].bitcast(FP8X4),
+                    lhsT_scale=scales[pair][:, samples],
+                    rhs=g_codes[n][:, g, 2 * first : 2 * (first + width)].bitcast(FP4X4),
+                    rhs_scale=g_scales[n][:, g, first : first + width],
                     start=(g == 0),
                     stop=False,
                 )
 
-        def new_pass(t, n, lo=0, width=N):
-            unit = "n%d" % (t // 2)
-            cols = slice(P * (t % 2), P * (t % 2 + 1))
+        def new_pass(t, n, first=0, width=N):
+            pair = ("new", t // 2)
+            samples = slice(P * (t % 2), P * (t % 2 + 1))
             nc.tensor.matmul_mx(
-                out=groups[t, n, lo][1][:, 0:width],
-                lhsT=codes[unit][:, cols].bitcast(FP8X4),
-                lhsT_scale=scales[unit][:, cols],
-                rhs=codes["g%d" % n][:, lo : lo + width].bitcast(FP8X4),
-                rhs_scale=scales["g%d" % n][:, lo : lo + width],
+                out=sums[t, n, first][1][:, 0:width],
+                lhsT=codes[pair][:, samples].bitcast(FP8X4),
+                lhsT_scale=scales[pair][:, samples],
+                rhs=codes["geno_new", n][:, first : first + width].bitcast(FP8X4),
+                rhs_scale=scales["geno_new", n][:, first : first + width],
                 start=False,
                 stop=True,
             )
 
-        shares = {}
-
-        def share(t, n):
-            tile = work.tile([P, N], F32, name="share", tag="share", bufs=8)
+        def sigmoid(t, n):
+            sigmoids[t, n] = work.tile([P, N], F32, name="sigmoid", tag="sigmoid", bufs=8)
             nc.scalar.activation(
-                out=tile[:], in_=ln_b[:, N * n : N * (n + 1)], func=ACT.Sigmoid, scale=-1.0, bias=ln_a[:, t : t + 1]
+                out=sigmoids[t, n][:],
+                in_=ln_b[:, N * n : N * (n + 1)],
+                func=ACT.Sigmoid,
+                scale=-1.0,
+                bias=ln_a[:, t : t + 1],
             )
-            shares[t, n] = tile
 
-        def finish(t, n, lo=0, width=N):
-            b, acc = groups[t, n, lo]
-            res = work.tile([P, width], F32, name="res", tag="res", bufs=16)
+        def finish(t, n, first=0, width=N):
+            number, bank = sums[t, n, first]
+            result = work.tile([P, width], F32, name="result", tag="result", bufs=RESULT_BUFS)
             nc.vector.scalar_tensor_tensor(
-                out=res[:],
-                in0=acc[:, 0:width],
+                out=result[:],
+                in0=bank[:, 0:width],
                 scalar=inv_a[:, t : t + 1],
-                in1=shares[t, n][:, lo : lo + width],
+                in1=sigmoids[t, n][:, first : first + width],
                 op0=ALU.mult,
                 op1=ALU.mult,
             )
-            free_banks.append(b)
-            nc.sync.dma_start(out=out_rows[t][:, N * n + lo : N * n + lo + width], in_=res[:])
+            free_banks.append(number)
+            nc.sync.dma_start(out=out_rows[t][:, N * n + first : N * n + first + width], in_=result[:])
 
-        cn_low_here = kept("cn_low_here", [P, 1], F32)
-        nc.vector.tensor_reduce(out=cn_low_here[:], in_=cn[:], axis=AXIS.X, op=ALU.min)
+        on_vector = nc.vector.tensor_copy
+        on_scalar = nc.scalar.copy
+
+        cn_min_here = kept("cn_min_here", [P, 1], F32)
+        nc.vector.tensor_reduce(out=cn_min_here[:], in_=cn[:], axis=AXIS.X, op=ALU.min)
         inv_rho = kept("inv_rho", [P, ROWS], F32)
         nc.vector.reciprocal(out=inv_rho[:], in_=rho[:])
-        low_b, low_bank = take_bank()
-        nc.tensor.transpose(low_bank[:, 0:P], cn_low_here[:, 0:1].to_broadcast([P, P]), ident[:])
+        min_number, min_bank = take_bank()
+        nc.tensor.transpose(min_bank[:, 0:P], cn_min_here[:, 0:1].to_broadcast([P, P]), ident[:])
         cn_words = cn[:].bitcast(F32)
         cn_banks = []
         for h in range(2):
-            b, bank = take_bank()
+            cn_banks.append(take_bank())
             for m in range(4):
                 word = cn_words[:, 4 * h + m : 4 * h + m + 1].to_broadcast([P, P])
-                nc.tensor.transpose(bank[:, P * m : P * (m + 1)], word, ident[:])
-            cn_banks.append((b, bank))
-        inv_rho_low = kept("inv_rho_low", [P, 1], F32)
-        nc.vector.tensor_reduce(out=inv_rho_low[:], in_=inv_rho[:], axis=AXIS.X, op=ALU.min)
-
-        cn_low = kept("cn_low", [P, 1], F32)
-        nc.vector.tensor_reduce(out=cn_low[:], in_=low_bank[:, 0:P], axis=AXIS.X, op=ALU.min)
-        free_banks.append(low_b)
+                nc.tensor.transpose(cn_banks[h][1][:, P * m : P * (m + 1)], word, ident[:])
+        inv_rho_min = kept("inv_rho_min", [P, 1], F32)
+        nc.vector.tensor_reduce(out=inv_rho_min[:], in_=inv_rho[:], axis=AXIS.X, op=ALU.min)
+        cn_min = kept("cn_min", [P, 1], F32)
+        nc.vector.tensor_reduce(out=cn_min[:], in_=min_bank[:, 0:P], axis=AXIS.X, op=ALU.min)
+        free_banks.append(min_number)
         shift = kept("shift", [P, 1], F32)
         nc.vector.scalar_tensor_tensor(
-            out=shift[:], in0=cn_low[:], scalar=-0.5, in1=inv_rho_low[:], op0=ALU.mult, op1=ALU.add
+            out=shift[:], in0=cn_min[:], scalar=-0.5, in1=inv_rho_min[:], op0=ALU.mult, op1=ALU.add
         )
-        order_words("k0", ["k0a", "k0b"])
+        sort_words(known_raw[0], known_pairs(0), on_vector)
         a = kept("a", [P, ROWS], F32)
         nc.vector.tensor_scalar(
             out=a[:], in0=inv_rho[:], scalar1=NORMAL, scalar2=shift[:, 0:1], op0=ALU.mult, op1=ALU.subtract
         )
         ln_b = kept("ln_b", [P, L], F32)
         for h in range(2):
-            b, bank = cn_banks[h]
+            number, bank = cn_banks[h]
             nc.scalar.activation(
                 out=ln_b[:].rearrange("q (p m e) -> q p m e", m=8, e=2)[:, :, 4 * h : 4 * h + 4, :],
                 in_=bank[:].bitcast(BF16).rearrange("q (m p e) -> q p m e", m=4, e=2),
                 func=ACT.Ln,
                 bias=shift[:, 0:1],
             )
-            free_banks.append(b)
+            free_banks.append(number)
         ln_a = kept("ln_a", [P, ROWS], F32)
         nc.scalar.activation(out=ln_a[:], in_=a[:], func=ACT.Ln)
-        turn("k0a")
-        turn("k0b")
-        order_words("k1", ["k1a", "k1b"])
-        turn("k1a")
-        turn("k1b")
-        gather("k0a", on_vector=True)
-        gather("k0b")
+
+        first_pairs = known_pairs(0) + known_pairs(1)
+        turn(first_pairs[0])
+        turn(first_pairs[1])
+        sort_words(known_raw[1], known_pairs(1), on_vector)
+        turn(first_pairs[2])
+        turn(first_pairs[3])
+        regroup(first_pairs[0], on_vector)
+        regroup(first_pairs[1], on_scalar)
         inv_a = kept("inv_a", [P, ROWS], F32)
         nc.vector.reciprocal(out=inv_a[:], in_=a[:])
-        quantise("k0a")
-        gather("k1a", on_vector=True)
-        quantise("k0b")
-        gather("k1b", on_vector=True)
-        quantise("k1a")
-        quantise("k1b")
-        for n in range(2):
-            for t in range(3):
-                share(t, n)
+        quantise(first_pairs[0])
+        regroup(first_pairs[2], on_vector)
+        quantise(first_pairs[1])
+        regroup(first_pairs[3], on_vector)
+        quantise(first_pairs[2])
+        quantise(first_pairs[3])
+
+        opening = [(t, n) for n in range(2) for t in range(3)]
+        for group in opening:
+            sigmoid(*group)
         known_passes(0, 0)
         known_passes(1, 0)
         known_passes(0, 1)
-        order_words("k2", ["k2a", "k2b"])
-        turn("k2a")
-        turn("k2b")
-        gather("k2a")
-        gather("k2b")
-        interleave_geno_new(0, N // 4)
-        order_words("n0", ["n0", "n1"])
-        quantise("k2a")
-        quantise("k2b")
-        quantise("g0")
+        sort_words(known_raw[2], known_pairs(2), on_vector)
+        for pair in known_pairs(2):
+            turn(pair)
+        for pair in known_pairs(2):
+            regroup(pair, on_scalar)
+        interleave_geno_new(0)
+        sort_words(new_raw[0], new_pairs(0), on_vector)
+        for pair in known_pairs(2):
+            quantise(pair)
+        quantise(("geno_new", 0))
         known_passes(1, 1)
-        turn("n0")
-        turn("n1")
-        gather("n0")
-        gather("n1")
+        for pair in new_pairs(0):
+            turn(pair)
+        for pair in new_pairs(0):
+            regroup(pair, on_scalar)
         known_passes(2, 0)
         known_passes(2, 1)
-        order_words("k3", ["k3a", "k3b"])
-        quantise("n0")
-        interleave_geno_new(1, SPLIT)
-        quantise("n1")
-        quantise("g1")
-        turn("k3a")
-        turn("k3b")
-        gather("k3a")
-        gather("k3b")
-        interleave_geno_new(2, SPLIT2)
-        closed = []
-        for n in range(2):
-            for t in range(3):
-                new_pass(t, n)
-                closed.append((t, n))
-        quantise("k3a")
-        finish(*closed[0])
-        closed.remove(closed[0])
-        quantise("k3b")
+        sort_words(known_raw[3], known_pairs(3), on_vector)
+        quantise(("new", 0))
+        interleave_geno_new(1)
+        quantise(("new", 1))
+        quantise(("geno_new", 1))
+        for pair in known_pairs(3):
+            turn(pair)
+        for pair in known_pairs(3):
+            regroup(pair, on_scalar)
+        interleave_geno_new(2)
+        for group in opening:
+            new_pass(*group)
+        quantise(("known", 3, 0))
+        finish(*opening[0])
+        quantise(("known", 3, 1))
+        closed = opening[1:]
 
         order = [(3, 0), (3, 1)]
         order.extend((t, 2) for t in range(4))
         order.extend((4, n) for n in range(3))
         order.extend((t, 3) for t in range(5))
         order.extend((t, n) for t in range(5, ROWS) for n in range(COLS))
-        col3 = order.index((0, 3))
-        share(*order[0])
-        share(*order[1])
-        for i, (t, n) in enumerate(order[:-1]):
-            for row in range(4, ROWS):
-                first = order.index((row, 0))
-                units = ["k%da" % row, "k%db" % row] + (["n%d" % (row // 2)] if row % 2 == 0 else [])
-                if i == first - 2:
-                    for unit in units:
-                        turn(unit)
-                    for unit in units:
-                        gather(unit)
-                if i == first - 1:
-                    for unit in units:
-                        quantise(unit)
+        last_block = order.index((0, COLS - 1))
+        vector_pairs = known_pairs(VECTOR_ROWS[0]) + known_pairs(VECTOR_ROWS[1])
+        block_steps = (sort_blocks, turn_blocks, regroup_blocks, quantise)
+        vector_start = order.index((VECTOR_ROWS[0], 0)) - len(block_steps) - 2 - SPARE_STEPS
+        sigmoid(*order[0])
+        sigmoid(*order[1])
+        for step, (t, n) in enumerate(order[:-1]):
+            for row in (4, 5):
+                pairs = known_pairs(row) + [("new", row - 2)]
+                if step == order.index((row, 0)) - 2:
+                    for pair in pairs:
+                        turn(pair)
+                    for pair in pairs:
+                        regroup(pair, on_scalar)
+                if step == order.index((row, 0)) - 1:
+                    for pair in pairs:
+                        quantise(pair)
             known_passes(t, n)
             new_pass(t, n)
-            for g in closed[:2]:
-                finish(*g)
-                closed.remove(g)
-                if g == G2AT:
-                    quantise("g2")
-            closed.append((t, n))
-            if i + 2 < len(order):
-                share(*order[i + 2])
-            for row in range(4, ROWS):
-                first = order.index((row, 0))
-                if i == first - 4:
-                    order_words("k%d" % row, ["k%da" % row, "k%db" % row], on_scalar=(row == 4))
-                if row == 4 and i == first - 3:
-                    order_words("n1", ["n2", "n3"], on_scalar=True)
-            if i == col3 - 3:
-                interleave_geno_new(3, N // 4)
-            if i == col3 - 2:
-                quantise("g3")
+            for group in closed[:2]:
+                finish(*group)
+                if group == (2, 0):
+                    quantise(("geno_new", 2))
+            closed = closed[2:] + [(t, n)]
+            if step + 2 < len(order):
+                sigmoid(*order[step + 2])
+            if step == order.index((4, 0)) - 4:
+                sort_words(known_raw[4], known_pairs(4), on_scalar)
+            if step == order.index((4, 0)) - 3:
+                sort_words(new_raw[1], new_pairs(1), on_scalar)
+            if step == order.index((5, 0)) - 4:
+                sort_words(known_raw[5], known_pairs(5), on_vector)
+            if step == last_block - 3:
+                interleave_geno_new(COLS - 1)
+            if step == last_block - 2:
+                quantise(("geno_new", COLS - 1))
+            for place, pair in enumerate(vector_pairs):
+                stage = step - vector_start - 2 * place
+                if 0 <= stage < len(block_steps):
+                    block_steps[stage](pair)
+
         t, n = order[-1]
-        for lo in range(0, N, P):
-            known_passes(t, n, lo, P)
-            new_pass(t, n, lo, P)
-            for g in closed[:]:
-                finish(*g)
-                closed.remove(g)
-            closed.append((t, n, lo, P))
+        for first in range(0, N, P):
+            known_passes(t, n, first, P)
+            new_pass(t, n, first, P)
+            for group in closed:
+                finish(*group)
+            closed = [(t, n, first, P)]
         finish(*closed[0])

from contextlib import ExitStack

import concourse.mybir as mybir
from concourse.masks import make_identity

S, C, U, L = 1024, 2048, 512, 2048
FLOPS = 2 * S * (C + U) * L

F32 = mybir.dt.float32
BF16 = mybir.dt.bfloat16
I32 = mybir.dt.int32
U32 = mybir.dt.uint32
U8 = mybir.dt.uint8
FP8X4 = mybir.dt.float8_e4m3fn_x4
FP4X4 = mybir.dt.float4_e2m1fn_x4
ALU = mybir.AluOpType
ACT = mybir.ActivationFunctionType
AXIS = mybir.AxisListType

P = 128
QUADRANT = 32
BANKS = 8
N = 512
ROWS = S // P
COLS = L // N
KNOWN_PASSES = C // 512
PAIR_WORDS = 512
NORMAL = 2.0

RUNS = N // 4
VECTOR_RUNS = (RUNS, 84, 64, RUNS)
VECTOR_ROWS = (ROWS - 2, ROWS - 1)
SPARE_STEPS = 2
RESULT_BUFS = 22


def tile_clone_allele_shift_s1_kernel(
    tc, d_known, geno_words, geno_scales, d_new, geno_new, purity, cn_excess, out
):
    nc = tc.nc
    known_rows = d_known.rearrange("(p t) k -> t p k", t=ROWS)
    new_rows = d_new.rearrange("(p t) k -> p (t k)", t=ROWS)
    out_rows = out.rearrange("(p t) n -> t p n", t=ROWS)

    with ExitStack() as ctx:
        keep = ctx.enter_context(tc.tile_pool(name="keep", bufs=1))
        work = ctx.enter_context(tc.tile_pool(name="work", bufs=3))
        psum = ctx.enter_context(tc.psum_pool(name="psum", bufs=1))
        ctx.enter_context(tc.manual_schedule())

        free_banks = list(range(BANKS))

        def take_bank():
            number = free_banks[0]
            free_banks.remove(number)
            return number, psum.tile([P, N], F32, name="bank%d" % number, tag="bank%d" % number)

        def kept(name, shape, dtype):
            return keep.tile(shape, dtype, name=name, tag=name, align_bytes=64)

        cn = kept("cn", [P, L // P], BF16)
        rho = kept("rho", [P, ROWS], BF16)
        nc.scalar.dma_start(out=cn[:], in_=cn_excess.rearrange("(p m) -> p m", p=P))
        nc.scalar.dma_start(out=rho[:], in_=purity.rearrange("(p t) -> p t", p=P))
        ident = kept("ident", [P, P], F32)
        make_identity(nc, ident[:])

        g_scales = []
        for n in range(COLS):
            scale_tile = kept("g_scales%d" % n, [P, KNOWN_PASSES, N], U8)
            nc.vector.memset(scale_tile[:].bitcast(I32), 0)
            g_scales.append(scale_tile)

        known_raw = {}
        new_raw = {}
        g_codes = {}
        geno_new_raw = {}

        def load_known(t):
            known_raw[t] = kept("known_raw%d" % t, [P, C], BF16)
            nc.sync.dma_start(out=known_raw[t][:], in_=known_rows[t])

        def load_new(half):
            new_raw[half] = kept("new_raw%d" % half, [P, 4 * U], BF16)
            nc.sync.dma_start(out=new_raw[half][:], in_=new_rows[:, 4 * U * half : 4 * U * (half + 1)])

        def load_g(n):
            for r in range(4):
                rows = geno_scales[:, r:16:4, N * n : N * (n + 1)].rearrange("g q n -> q g n")
                nc.sync.dma_start(out=g_scales[n][r:P:QUADRANT, :, :].bitcast(I32), in_=rows.bitcast(I32))
            g_codes[n] = kept("g_codes%d" % n, [P, KNOWN_PASSES, 2 * N], U8)
            words = geno_words[:, :, 2 * N * n : 2 * N * (n + 1)].rearrange("g p b -> p g b")
            nc.sync.dma_start(out=g_codes[n][:].bitcast(I32), in_=words.bitcast(I32))

        def load_geno_new(n):
            geno_new_raw[n] = kept("geno_new_raw%d" % n, [P, 4, N], BF16)
            rows = geno_new[:, N * n : N * (n + 1)].rearrange("(p j) w -> p j w", j=4)
            nc.sync.dma_start(out=geno_new_raw[n][:], in_=rows)

        load_known(0)
        load_known(1)
        load_g(0)
        load_g(1)
        load_known(2)
        load_geno_new(0)
        load_new(0)
        load_known(3)
        load_geno_new(1)
        load_geno_new(2)
        load_g(2)
        load_known(4)
        load_new(1)
        load_geno_new(3)
        load_g(3)
        load_known(5)
        by_quadrant = kept("by_quadrant", [P, 4, 2 * KNOWN_PASSES, P], BF16)
        pieces = d_known.rearrange("(i b t) (g q k) -> b q i (t g) k", b=4, t=ROWS, q=4, k=P)
        for b in range(4):
            for q in (0, 2, 1, 3):
                nc.sync.dma_start(
                    out=by_quadrant[QUADRANT * q : QUADRANT * (q + 1), b, :, :],
                    in_=pieces[b, q][:, KNOWN_PASSES * VECTOR_ROWS[0] :, :],
                )

        sorted_words = {}
        turned = {}
        grouped = {}
        codes = {}
        scales = {}

        def known_pairs(t):
            return [("known", t, 0), ("known", t, 1)]

        def new_pairs(half):
            return [("new", 2 * half), ("new", 2 * half + 1)]

        def sort_words(raw, pairs, copy):
            tile = work.tile([P, 2 * PAIR_WORDS], F32, name="sorted", tag="sorted", bufs=3, align_bytes=64)
            copy(
                out=tile[:].rearrange("p (g u c i) -> p g c u i", u=2, c=32, i=4),
                in_=raw[:].bitcast(F32).rearrange("p (g c i u) -> p g c u i", u=2, c=32, i=4),
            )
            for place, pair in enumerate(pairs):
                sorted_words[pair] = tile[:, PAIR_WORDS * place : PAIR_WORDS * (place + 1)]

        def turn(pair):
            number, bank = take_bank()
            for x in range(4):
                nc.tensor.transpose(bank[:, P * x : P * (x + 1)], sorted_words[pair][:, P * x : P * (x + 1)], ident[:])
            turned[pair] = (number, bank)

        def group_tile():
            return work.tile([P, 2 * PAIR_WORDS], BF16, name="grouped", tag="grouped", bufs=6, align_bytes=64)

        def regroup(pair, copy):
            number, bank = turned[pair]
            grouped[pair] = group_tile()
            copy(
                out=grouped[pair][:].bitcast(F32).rearrange("p (g m u) -> p g m u", g=2, u=2),
                in_=bank[:].rearrange("p (g u m) -> p g m u", g=2, u=2),
            )
            free_banks.append(number)

        def sort_blocks(pair):
            place, half = VECTOR_ROWS.index(pair[1]), pair[2]
            tile = work.tile([P, PAIR_WORDS], F32, name="sorted_blocks", tag="sorted_blocks", align_bytes=64)
            words = by_quadrant[:].rearrange("p b x k -> p (b x k)").bitcast(F32)
            words = words.rearrange("p (b v g j u) -> p v g b u j", b=4, v=2, g=KNOWN_PASSES, u=2)
            nc.scalar.copy(
                out=tile[:].rearrange("p (g b u j) -> p g b u j", g=2, b=4, u=2),
                in_=words[:, place, 2 * half : 2 * half + 2],
            )
            sorted_words[pair] = tile

        def turn_blocks(pair):
            turned[pair] = work.tile([P, PAIR_WORDS], F32, name="turned_blocks", tag="turned_blocks", align_bytes=64)
            nc.vector.transpose(out=turned[pair][:], in_=sorted_words[pair][:])

        def regroup_blocks(pair):
            grouped[pair] = group_tile()
            nc.scalar.copy(
                out=grouped[pair][:].bitcast(F32).rearrange("p (g i c x) -> p g c i x", g=2, c=2, x=4),
                in_=turned[pair][:].rearrange("p (g c x i) -> p g c i x", g=2, c=2, x=4),
            )

        def interleave_geno_new(n):
            tile = work.tile([P, 4 * N], BF16, name="interleaved", tag="interleaved", bufs=2, align_bytes=64)
            dst = tile[:].rearrange("p (c i j) -> p c j i", i=4, j=4)
            src = geno_new_raw[n][:].rearrange("p j (c i) -> p c j i", i=4)
            split = VECTOR_RUNS[n]
            nc.vector.tensor_copy(out=dst[:, 0:split], in_=src[:, 0:split])
            if split < RUNS:
                nc.scalar.copy(out=dst[:, split:], in_=src[:, split:])
            grouped["geno_new", n] = tile

        def quantise(key):
            columns = grouped[key].shape[1] // 4
            name = "_".join(str(part) for part in key)
            codes[key] = kept("codes_" + name, [P, columns], U32)
            scales[key] = kept("scales_" + name, [P, columns], U8)
            nc.vector.quantize_mx(out=codes[key][:].bitcast(FP8X4), scales=scales[key][:], in_=grouped[key][:])

        sums = {}
        sigmoids = {}

        def known_passes(t, n, first=0, width=N):
            sums[t, n, first] = take_bank()
            for g in range(KNOWN_PASSES):
                pair = ("known", t, g // 2)
                samples = slice(P * (g % 2), P * (g % 2 + 1))
                nc.tensor.matmul_mx(
                    out=sums[t, n, first][1][:, 0:width],
                    lhsT=codes[pair][:, samples].bitcast(FP8X4),
                    lhsT_scale=scales[pair][:, samples],
                    rhs=g_codes[n][:, g, 2 * first : 2 * (first + width)].bitcast(FP4X4),
                    rhs_scale=g_scales[n][:, g, first : first + width],
                    start=(g == 0),
                    stop=False,
                )

        def new_pass(t, n, first=0, width=N):
            pair = ("new", t // 2)
            samples = slice(P * (t % 2), P * (t % 2 + 1))
            nc.tensor.matmul_mx(
                out=sums[t, n, first][1][:, 0:width],
                lhsT=codes[pair][:, samples].bitcast(FP8X4),
                lhsT_scale=scales[pair][:, samples],
                rhs=codes["geno_new", n][:, first : first + width].bitcast(FP8X4),
                rhs_scale=scales["geno_new", n][:, first : first + width],
                start=False,
                stop=True,
            )

        def sigmoid(t, n):
            sigmoids[t, n] = work.tile([P, N], F32, name="sigmoid", tag="sigmoid", bufs=8)
            nc.scalar.activation(
                out=sigmoids[t, n][:],
                in_=ln_b[:, N * n : N * (n + 1)],
                func=ACT.Sigmoid,
                scale=-1.0,
                bias=ln_a[:, t : t + 1],
            )

        def finish(t, n, first=0, width=N):
            number, bank = sums[t, n, first]
            result = work.tile([P, width], F32, name="result", tag="result", bufs=RESULT_BUFS)
            nc.vector.scalar_tensor_tensor(
                out=result[:],
                in0=bank[:, 0:width],
                scalar=inv_a[:, t : t + 1],
                in1=sigmoids[t, n][:, first : first + width],
                op0=ALU.mult,
                op1=ALU.mult,
            )
            free_banks.append(number)
            nc.sync.dma_start(out=out_rows[t][:, N * n + first : N * n + first + width], in_=result[:])

        on_vector = nc.vector.tensor_copy
        on_scalar = nc.scalar.copy

        cn_min_here = kept("cn_min_here", [P, 1], F32)
        nc.vector.tensor_reduce(out=cn_min_here[:], in_=cn[:], axis=AXIS.X, op=ALU.min)
        inv_rho = kept("inv_rho", [P, ROWS], F32)
        nc.vector.reciprocal(out=inv_rho[:], in_=rho[:])
        min_number, min_bank = take_bank()
        nc.tensor.transpose(min_bank[:, 0:P], cn_min_here[:, 0:1].to_broadcast([P, P]), ident[:])
        cn_words = cn[:].bitcast(F32)
        cn_banks = []
        for h in range(2):
            cn_banks.append(take_bank())
            for m in range(4):
                word = cn_words[:, 4 * h + m : 4 * h + m + 1].to_broadcast([P, P])
                nc.tensor.transpose(cn_banks[h][1][:, P * m : P * (m + 1)], word, ident[:])
        inv_rho_min = kept("inv_rho_min", [P, 1], F32)
        nc.vector.tensor_reduce(out=inv_rho_min[:], in_=inv_rho[:], axis=AXIS.X, op=ALU.min)
        cn_min = kept("cn_min", [P, 1], F32)
        nc.vector.tensor_reduce(out=cn_min[:], in_=min_bank[:, 0:P], axis=AXIS.X, op=ALU.min)
        free_banks.append(min_number)
        shift = kept("shift", [P, 1], F32)
        nc.vector.scalar_tensor_tensor(
            out=shift[:], in0=cn_min[:], scalar=-0.5, in1=inv_rho_min[:], op0=ALU.mult, op1=ALU.add
        )
        sort_words(known_raw[0], known_pairs(0), on_vector)
        a = kept("a", [P, ROWS], F32)
        nc.vector.tensor_scalar(
            out=a[:], in0=inv_rho[:], scalar1=NORMAL, scalar2=shift[:, 0:1], op0=ALU.mult, op1=ALU.subtract
        )
        ln_b = kept("ln_b", [P, L], F32)
        for h in range(2):
            number, bank = cn_banks[h]
            nc.scalar.activation(
                out=ln_b[:].rearrange("q (p m e) -> q p m e", m=8, e=2)[:, :, 4 * h : 4 * h + 4, :],
                in_=bank[:].bitcast(BF16).rearrange("q (m p e) -> q p m e", m=4, e=2),
                func=ACT.Ln,
                bias=shift[:, 0:1],
            )
            free_banks.append(number)
        ln_a = kept("ln_a", [P, ROWS], F32)
        nc.scalar.activation(out=ln_a[:], in_=a[:], func=ACT.Ln)

        first_pairs = known_pairs(0) + known_pairs(1)
        turn(first_pairs[0])
        turn(first_pairs[1])
        sort_words(known_raw[1], known_pairs(1), on_vector)
        turn(first_pairs[2])
        turn(first_pairs[3])
        regroup(first_pairs[0], on_vector)
        regroup(first_pairs[1], on_scalar)
        inv_a = kept("inv_a", [P, ROWS], F32)
        nc.vector.reciprocal(out=inv_a[:], in_=a[:])
        quantise(first_pairs[0])
        regroup(first_pairs[2], on_vector)
        quantise(first_pairs[1])
        regroup(first_pairs[3], on_vector)
        quantise(first_pairs[2])
        quantise(first_pairs[3])

        opening = [(t, n) for n in range(2) for t in range(3)]
        for group in opening:
            sigmoid(*group)
        known_passes(0, 0)
        known_passes(1, 0)
        known_passes(0, 1)
        sort_words(known_raw[2], known_pairs(2), on_vector)
        for pair in known_pairs(2):
            turn(pair)
        for pair in known_pairs(2):
            regroup(pair, on_scalar)
        interleave_geno_new(0)
        sort_words(new_raw[0], new_pairs(0), on_vector)
        for pair in known_pairs(2):
            quantise(pair)
        quantise(("geno_new", 0))
        known_passes(1, 1)
        for pair in new_pairs(0):
            turn(pair)
        for pair in new_pairs(0):
            regroup(pair, on_scalar)
        known_passes(2, 0)
        known_passes(2, 1)
        sort_words(known_raw[3], known_pairs(3), on_vector)
        quantise(("new", 0))
        interleave_geno_new(1)
        quantise(("new", 1))
        quantise(("geno_new", 1))
        for pair in known_pairs(3):
            turn(pair)
        for pair in known_pairs(3):
            regroup(pair, on_scalar)
        interleave_geno_new(2)
        for group in opening:
            new_pass(*group)
        quantise(("known", 3, 0))
        finish(*opening[0])
        quantise(("known", 3, 1))
        closed = opening[1:]

        order = [(3, 0), (3, 1)]
        order.extend((t, 2) for t in range(4))
        order.extend((4, n) for n in range(3))
        order.extend((t, 3) for t in range(5))
        order.extend((t, n) for t in range(5, ROWS) for n in range(COLS))
        last_block = order.index((0, COLS - 1))
        vector_pairs = known_pairs(VECTOR_ROWS[0]) + known_pairs(VECTOR_ROWS[1])
        block_steps = (sort_blocks, turn_blocks, regroup_blocks, quantise)
        vector_start = order.index((VECTOR_ROWS[0], 0)) - len(block_steps) - 2 - SPARE_STEPS
        sigmoid(*order[0])
        sigmoid(*order[1])
        for step, (t, n) in enumerate(order[:-1]):
            for row in (4, 5):
                pairs = known_pairs(row) + [("new", row - 2)]
                if step == order.index((row, 0)) - 2:
                    for pair in pairs:
                        turn(pair)
                    for pair in pairs:
                        regroup(pair, on_scalar)
                if step == order.index((row, 0)) - 1:
                    for pair in pairs:
                        quantise(pair)
            known_passes(t, n)
            new_pass(t, n)
            for group in closed[:2]:
                finish(*group)
                if group == (2, 0):
                    quantise(("geno_new", 2))
            closed = closed[2:] + [(t, n)]
            if step + 2 < len(order):
                sigmoid(*order[step + 2])
            if step == order.index((4, 0)) - 4:
                sort_words(known_raw[4], known_pairs(4), on_scalar)
            if step == order.index((4, 0)) - 3:
                sort_words(new_raw[1], new_pairs(1), on_scalar)
            if step == order.index((5, 0)) - 4:
                sort_words(known_raw[5], known_pairs(5), on_vector)
            if step == last_block - 3:
                interleave_geno_new(COLS - 1)
            if step == last_block - 2:
                quantise(("geno_new", COLS - 1))
            for place, pair in enumerate(vector_pairs):
                stage = step - vector_start - 2 * place
                if 0 <= stage < len(block_steps):
                    block_steps[stage](pair)

        t, n = order[-1]
        for first in range(0, N, P):
            known_passes(t, n, first, P)
            new_pass(t, n, first, P)
            for group in closed:
                finish(*group)
            closed = [(t, n, first, P)]
        finish(*closed[0])
